import numpy as np
import ml_dtypes


def mxq(x, axis, fmt="e4m3"):
    dtype, down = {"e4m3": (ml_dtypes.float8_e4m3fn, 7), "e5m2": (ml_dtypes.float8_e5m2, 14)}[fmt]
    v = np.moveaxis(np.asarray(x, np.float32).astype(ml_dtypes.bfloat16).astype(np.float64), axis, -1)
    blocks = v.reshape(v.shape[:-1] + (-1, 32))
    amax = np.abs(blocks).max(-1, keepdims=True)
    byte = np.maximum(np.where(amax > 0, np.frexp(amax)[1] - 1 + 127, 0) - down, 1)
    scale = np.exp2(byte - 127.0)
    codes = (blocks / scale).astype(np.float32).astype(dtype).astype(np.float64)
    return np.moveaxis((codes * scale).reshape(v.shape), -1, axis)


WIDE = False


def mx_kscale(k):
    if not WIDE:
        return np.ones(k)
    levels = np.array([10, -10, 5, -5, 0])
    if k % 512:
        return np.exp2(np.random.permutation(np.resize(levels, k // 32))).repeat(32)
    a = np.empty((k // 512, 16))
    for p in range(k // 512):
        a[p, :8] = np.random.permutation(np.resize(levels, 8))
        for g in range(8):
            far = levels[np.abs(levels - a[p, g]) >= 10]
            a[p, g + 8] = far[np.random.randint(len(far))]
    return np.exp2(a.ravel()).repeat(32)


BF16 = ml_dtypes.bfloat16


def bf(x):
    return np.asarray(x, np.float32).astype(BF16)


def f64(x):
    return np.asarray(x).astype(np.float64)


E2M1 = np.array([0.0, 0.5, 1.0, 1.5, 2.0, 3.0, 4.0, 6.0, -0.0, -0.5, -1.0, -1.5, -2.0, -3.0, -4.0, -6.0])


def pack_weight(w, fmt):
    k, n = w.shape
    w = f64(bf(w)).reshape(k // 32, 32, n)
    amax = np.abs(w).max(1)
    if fmt == "e4m3":
        byte = np.frexp(amax)[1] - 1 + 127 - 7
    else:
        mant, ex = np.frexp(amax / 6.0)
        byte = np.where(mant > 0.5, ex, ex - 1) + 127
    byte = np.clip(np.where(amax > 0, byte, 1), 1, 254)
    scaled = (w * np.exp2(127.0 - byte)[:, None, :]).reshape(k, n).astype(np.float32)
    by_word = np.ascontiguousarray(scaled.reshape(k // 512, 128, 4, n).transpose(0, 1, 3, 2))
    if fmt == "e4m3":
        words = by_word.astype(ml_dtypes.float8_e4m3fn).view(np.uint8)
    else:
        c = by_word.astype(ml_dtypes.float4_e2m1fn).view(np.uint8) & 0xF
        words = c[..., 0::2] | (c[..., 1::2] << 4)
    return np.ascontiguousarray(words), np.ascontiguousarray(byte.astype(np.uint8).reshape(k // 512, 16, n))


def unpack_weight(words, scales, fmt):
    g, p, n, _ = words.shape
    if fmt == "e4m3":
        vals = np.ascontiguousarray(words).view(ml_dtypes.float8_e4m3fn).astype(np.float64)
    else:
        nib = np.empty((g, p, n, 4), np.uint8)
        nib[..., 0::2] = words & 0xF
        nib[..., 1::2] = words >> 4
        vals = E2M1[nib]
    vals = vals * np.repeat(np.exp2(scales.astype(np.float64) - 127.0), 8, axis=1)[..., None]
    return vals.transpose(0, 1, 3, 2).reshape(g * 512, n)

E4M3FN = np.array([(-1.0 if i & 128 else 1.0) * ((1.0 + (i & 7) / 8.0) * 2.0 ** (((i >> 3) & 15) - 7) if i & 120 else (i & 7) * 2.0 ** -9) for i in range(256)])


def e4m3fn_bytes(y):
    return np.clip(np.asarray(y, np.float64), -448.0, 448.0).astype(np.float32).astype(ml_dtypes.float8_e4m3fn).view(np.uint8)


def e4m3fn_values(b):
    return E4M3FN[b]


N, D, E = 512, 1024, 512
D2 = 2 * D

DT = 0.5
GAM = 1.0
EPS = 0.5


def draw0():
    s = mx_kscale(E)
    t = mx_kscale(D2)
    y0 = bf(np.random.standard_normal((N, D)))
    z0 = bf(np.random.standard_normal((N, D)))
    u = bf(np.random.standard_normal((N, E)) * s)
    w_words, w_scales = pack_weight(np.random.standard_normal((D2, D)) / np.sqrt(D2) / t[:, None], "e4m3")
    v_words, v_scales = pack_weight(np.random.standard_normal((E, D)) / np.sqrt(E) / s[:, None], "e4m3")
    return {
        "y0": y0,
        "z0": z0,
        "u": u,
        "w_words": w_words,
        "w_scales": w_scales,
        "v_words": v_words,
        "v_scales": v_scales,
        "b": bf(np.random.standard_normal(D) * 0.4),
        "g": bf((1.0 + 0.25 * np.random.standard_normal(D2)) * t),
    }


def _substep(y, z, d, wq, g):
    s = np.concatenate([y, z], axis=-1) * g
    z_new = z + DT * (np.tanh((mxq(s, 1, "e4m3") @ wq) + d) - GAM * y - EPS * z)
    y_new = y + DT * z_new
    return y_new, z_new


def core(y0, z0, u, w_words, w_scales, v_words, v_scales, b, g):
    wq = unpack_weight(w_words, w_scales, "e4m3")
    gain = f64(g)
    d = (mxq(f64(u), 1, "e4m3") @ unpack_weight(v_words, v_scales, "e4m3")) + f64(b)
    y1, z1 = _substep(f64(y0), f64(z0), d, wq, gain)
    y2, z2 = _substep(y1, z1, d, wq, gain)
    return y2, z2


def setup_inputs():
    drawn = draw0()
    full = np.asarray(drawn['u']).astype(np.float64)
    scale = (np.abs(full).reshape(512, 4, 128).max(axis=(2,)) / 448.0).astype(np.float32)
    given = {}
    for key, value in drawn.items():
        if key == 'u':
            given['u_bytes'] = e4m3fn_bytes(full / np.repeat(scale.astype(np.float64), 128, axis=1))
            given['u_scale'] = scale
        else:
            given[key] = value
    return given


def reference(y0, z0, u_bytes, u_scale, w_words, w_scales, v_words, v_scales, b, g):
    return core(y0, z0, e4m3fn_values(u_bytes) * np.repeat(u_scale.astype(np.float64), 128, axis=1), w_words, w_scales, v_words, v_scales, b, g)

@@ -1,0 +1,358 @@
+from contextlib import ExitStack
+
+import concourse.mybir as mybir
+from concourse.masks import make_identity
+
+N, D, E = 512, 1024, 512
+D2 = 2 * D
+FLOPS = 2 * N * D * (E + 2 * D2)
+
+F32 = mybir.dt.float32
+BF16 = mybir.dt.bfloat16
+I32 = mybir.dt.int32
+U8 = mybir.dt.uint8
+FP8 = mybir.dt.float8_e4m3fn
+FP8X4 = mybir.dt.float8_e4m3fn_x4
+ALU = mybir.AluOpType
+ACT = mybir.ActivationFunctionType
+
+P = 128
+TC = 256
+CHUNKS = N // TC
+TT = TC // P
+ORDER = {1: (0, 1, 2, 3, "u"), 2: ("u", 0, 2, 1, 3)}
+
+
+def tile_coupledoscillatorrnntwosubsteps_d1p_kernel(
+    tc, y0, z0, u_bytes, u_scale, w_words, w_scales, v_words, v_scales, b, g, out_0, out_1
+):
+    nc = tc.nc
+    with ExitStack() as ctx:
+        keep = ctx.enter_context(tc.tile_pool(name="keep", bufs=1))
+        ring = ctx.enter_context(tc.tile_pool(name="ring", bufs=2))
+        psum = ctx.enter_context(tc.psum_pool(name="psum", bufs=1))
+
+        def sb(name, shape, dtype):
+            return keep.tile(shape, dtype, name=name, align_bytes=64)
+
+        sc_raw = sb("sc_raw", [P, 2, D], U8)
+        nc.vector.memset(sc_raw[:].rearrange("p x n -> p (x n)").bitcast(I32), 0)
+        ident = sb("ident", [P, P], F32)
+        make_identity(nc, ident[:])
+
+        us = sb("us", [P, 4, 4], F32)
+        nc.scalar.dma_start(out=us[:], in_=u_scale.rearrange("(i p) j -> p i j", p=P))
+        gb = sb("gb", [P, 4, 4], BF16)
+        nc.scalar.dma_start(out=gb[:], in_=g.rearrange("(q p t) -> p q t", p=P, t=4))
+        bb = sb("bb", [P, 2, 4], BF16)
+        nc.scalar.dma_start(out=bb[:], in_=b.rearrange("(q p t) -> p q t", p=P, t=4))
+
+        w_raw = sb("w_raw", [P, 4, D], I32)
+        v_raw = sb("v_raw", [P, D], I32)
+        w_view = w_words.rearrange("q p n t -> p q (n t)")
+        v_view = v_words[0].rearrange("p n t -> p (n t)")
+        y_view = y0.rearrange("(i p) d -> p i d", p=P)
+        z_view = z0.rearrange("(i p) d -> p i d", p=P)
+        y_nat = sb("y_nat", [P, 4, D], BF16)
+        z_nat = sb("z_nat", [P, 4, D], BF16)
+        u_raw = sb("u_raw", [P, 4, E], U8)
+
+        def load_w(h, q):
+            nc.sync.dma_start(
+                out=w_raw[:, q : q + 2, 512 * h : 512 * h + 512],
+                in_=w_view[:, q : q + 2, 2048 * h : 2048 * h + 2048].bitcast(I32),
+            )
+
+        def load_v(h):
+            nc.sync.dma_start(
+                out=v_raw[:, 512 * h : 512 * h + 512], in_=v_view[:, 2048 * h : 2048 * h + 2048].bitcast(I32)
+            )
+
+        nc.sync.dma_start(out=y_nat[:, 0:2, :], in_=y_view[:, 0:2, :])
+        load_w(0, 0)
+        nc.sync.dma_start(out=u_raw[:], in_=u_bytes.rearrange("(i p) k -> p i k", p=P))
+        nc.sync.dma_start(out=z_nat[:, 0:2, :], in_=z_view[:, 0:2, :])
+        load_w(0, 2)
+        load_v(0)
+        for q in range(4):
+            nc.sync.dma_start(
+                out=sc_raw[32 * q : 32 * q + 16, 0, :].bitcast(I32),
+                in_=w_scales[:, 4 * q : 4 * q + 4, :].bitcast(I32),
+            )
+        for q in range(4):
+            nc.gpsimd.dma_start(
+                out=sc_raw[32 * q : 32 * q + 4, 1, :].bitcast(I32),
+                in_=v_scales[0, 4 * q : 4 * q + 4, :].bitcast(I32),
+            )
+        load_w(1, 0)
+        load_w(1, 2)
+        load_v(1)
+        nc.sync.dma_start(out=y_nat[:, 2:4, :], in_=y_view[:, 2:4, :])
+        nc.sync.dma_start(out=z_nat[:, 2:4, :], in_=z_view[:, 2:4, :])
+
+        eye75 = sb("eye75", [P, P], BF16)
+        nc.vector.tensor_scalar(out=eye75[:], in0=ident[:], scalar1=0.75, scalar2=None, op0=ALU.mult)
+        eyem5 = sb("eyem5", [P, P], BF16)
+        nc.vector.tensor_scalar(out=eyem5[:], in0=ident[:], scalar1=-0.5, scalar2=None, op0=ALU.mult)
+
+        gf = sb("gf", [P, 4, 4], F32)
+        bf = sb("bf", [P, 8], F32)
+
+        def small_casts():
+            nc.vector.tensor_copy(out=gf[:], in_=gb[:])
+            nc.vector.tensor_copy(out=bf[:], in_=bb[:].rearrange("p q t -> p (q t)"))
+
+        def gain(q):
+            return gb[:, q, :].unsqueeze(1).to_broadcast([P, TC, 4])
+
+        wp = sb("wp", [P, 4, D], I32)
+        vp = sb("vp", [P, D], I32)
+        scp = sb("scp", [P, 2, D], U8)
+
+        def permute_scales(x):
+            nc.vector.tensor_copy(
+                out=scp[:, x, :].rearrange("p (h t m) -> p h t m", h=2, t=4),
+                in_=sc_raw[:, x, :].rearrange("p (h m t) -> p h t m", h=2, t=4),
+            )
+
+        def permute_w(h, qs):
+            cols = slice(512 * h, 512 * h + 512)
+            for q in qs:
+                nc.vector.tensor_copy(
+                    out=wp[:, q, cols].rearrange("p (t m) -> p t m", t=4),
+                    in_=w_raw[:, q, cols].rearrange("p (m t) -> p t m", t=4),
+                )
+
+        def permute_v(h):
+            cols = slice(512 * h, 512 * h + 512)
+            nc.vector.tensor_copy(
+                out=vp[:, cols].rearrange("p (t m) -> p t m", t=4),
+                in_=v_raw[:, cols].rearrange("p (m t) -> p t m", t=4),
+            )
+
+        u_wide = sb("u_wide", [P, 4, E], BF16)
+
+        def widen_u(i):
+            for j in range(4):
+                nc.scalar.activation(
+                    out=u_wide[:, i, 128 * j : 128 * j + 128],
+                    in_=u_raw[:, i, 128 * j : 128 * j + 128].bitcast(FP8),
+                    func=ACT.Copy,
+                    scale=us[:, i, j : j + 1],
+                )
+
+        def words_transposed(dst, nat, c, q, copy=nc.scalar.copy):
+            bank = psum.tile([P, TT, 2, P], F32, name="tp", bufs=2)
+            for i in range(TT):
+                words = nat[:, TT * c + i, :].bitcast(F32)
+                for e in range(2):
+                    nc.tensor.transpose(bank[:, i, e, :], words[:, 256 * q + e : 256 * (q + 1) : 2], ident[:])
+            copy(
+                out=dst.rearrange("p (i r) t -> p i (r t)", i=TT).bitcast(F32).rearrange("p i (r e) -> p i r e", e=2),
+                in_=bank[:].rearrange("p i e r -> p i r e"),
+            )
+
+        u_q = sb("u_q", [P, CHUNKS, TC], I32)
+        u_s = sb("u_s", [P, CHUNKS, TC], U8)
+
+        def make_u(c):
+            ut = ring.tile([P, TC, 4], BF16, name="ut", align_bytes=64)
+            words_transposed(ut[:], u_wide, c, 0)
+            nc.vector.quantize_mx(
+                out=u_q[:, c, :].bitcast(FP8X4), scales=u_s[:, c, :], in_=ut[:].rearrange("p n t -> p (n t)")
+            )
+
+        raw = {}
+        s_q = {}
+        s_s = {}
+        for k in (1, 2):
+            for c in range(CHUNKS):
+                s_q[k, c] = sb("sq%d%d" % (k, c), [P, 4, TC], I32)
+                s_s[k, c] = sb("ss%d%d" % (k, c), [P, 4, TC], U8)
+
+        def quantize(k, c, q, s):
+            nc.vector.quantize_mx(
+                out=s_q[k, c][:, q, :].bitcast(FP8X4), scales=s_s[k, c][:, q, :], in_=s[:].rearrange("p n t -> p (n t)")
+            )
+
+        def transpose_in(c, qs):
+            for q in qs:
+                nat = y_nat if q < 2 else z_nat
+                raw[c, q] = sb("raw%d%d" % (c, q), [P, TC, 4], BF16)
+                words_transposed(raw[c, q][:], nat, c, q % 2, copy=nc.vector.tensor_copy if (c == 0 and q == 3) else nc.scalar.copy)
+
+        def gain_and_quantize(c, qs):
+            tiles = []
+            for q in qs:
+                s = ring.tile([P, TC, 4], BF16, name="s1", bufs=4, align_bytes=64)
+                nc.vector.tensor_tensor(out=s[:], in0=raw[c, q][:], in1=gain(q), op=ALU.mult)
+                tiles.append(s)
+            for q, s in zip(qs, tiles):
+                quantize(1, c, q, s)
+
+        def mx_passes(out, j, k, c, passes):
+            cols = slice(128 * j, 128 * j + 128)
+            order = ORDER[k]
+            for q in passes:
+                if q == "u":
+                    lhsT, lhsT_scale, rhs, rhs_scale = vp[:, cols], scp[:, 1, cols], u_q[:, c, :], u_s[:, c, :]
+                else:
+                    lhsT, lhsT_scale = wp[:, q, cols], scp[4 * q : P, 0, cols]
+                    rhs, rhs_scale = s_q[k, c][:, q, :], s_s[k, c][:, q, :]
+                nc.tensor.matmul_mx(
+                    out=out, lhsT=lhsT.bitcast(FP8X4), lhsT_scale=lhsT_scale, rhs=rhs.bitcast(FP8X4), rhs_scale=rhs_scale,
+                    start=(q == order[0]), stop=(q == order[-1]),
+                )
+
+        t1 = {}
+        z1 = {}
+        y1 = {}
+        t2 = {}
+        zb = {}
+        yb = {}
+        mb = {}
+
+        def matmuls(k, c, h, early=False):
+            if k == 1:
+                t = t1[c, h] = ring.tile([P, 4, TC], F32, name="t1", bufs=4)
+            else:
+                t = t2[c, h] = sb("t2_%d%d" % (c, h), [P, 4, TC], F32)
+            banks = [psum.tile([P, 2, TC], F32, name="mx", bufs=2) for i in range(2)]
+            if early:
+                for i in range(2):
+                    mx_passes(banks[i][:, 0, :], 4 * h + 2 * i, k, c, ORDER[k][:3])
+            for i in range(2):
+                bank = banks[i]
+                for e in range(2):
+                    mx_passes(bank[:, e, :], 4 * h + 2 * i + e, k, c, ORDER[k][3:] if early and e == 0 else ORDER[k])
+                for e in range(2):
+                    j = 4 * h + 2 * i + e
+                    nc.scalar.activation(out=t[:, 2 * i + e, :], in_=bank[:, e, :], func=ACT.Tanh, bias=bf[:, j : j + 1])
+
+        def drift(c, h):
+            for i in range(2):
+                m = mb[c, h, i] = psum.tile([P, 2, TC], F32, name="mb", bufs=4)
+                for e in range(2):
+                    t = 2 * i + e
+                    nc.tensor.matmul(m[:, e, :], lhsT=eye75[:], rhs=raw[c, 2 + h][:, :, t], start=True, stop=False)
+                    nc.tensor.matmul(m[:, e, :], lhsT=eyem5[:], rhs=raw[c, h][:, :, t], start=False, stop=True)
+
+        def state(c, h):
+            z = z1[c, h] = sb("z1_%d%d" % (c, h), [P, 4, TC], F32)
+            y = y1[c, h] = sb("y1_%d%d" % (c, h), [P, 4, TC], F32)
+            zb[c, h] = ring.tile([P, 4, TC], BF16, name="zb")
+            yb[c, h] = ring.tile([P, 4, TC], BF16, name="yb")
+            for i in range(2):
+                pair = slice(2 * i, 2 * i + 2)
+                nc.vector.scalar_tensor_tensor(
+                    out=z[:, pair, :], in0=t1[c, h][:, pair, :], scalar=0.5, in1=mb[c, h, i][:], op0=ALU.mult, op1=ALU.add
+                )
+            for t in range(4):
+                nc.scalar.activation(out=zb[c, h][:, t, :], in_=z[:, t, :], func=ACT.Copy, scale=gf[:, 2 + h, t : t + 1])
+            for i in range(2):
+                pair = slice(2 * i, 2 * i + 2)
+                nc.vector.scalar_tensor_tensor(
+                    out=y[:, pair, :], in0=z[:, pair, :], scalar=0.5,
+                    in1=raw[c, h][:].rearrange("p n t -> p t n")[:, pair, :], op0=ALU.mult, op1=ALU.add,
+                )
+            for t in range(4):
+                nc.scalar.activation(out=yb[c, h][:, t, :], in_=y[:, t, :], func=ACT.Copy, scale=gf[:, h, t : t + 1])
+
+        def second_operand(c, h):
+            sz = ring.tile([P, TC, 4], BF16, name="sz", align_bytes=64)
+            nc.vector.tensor_copy(out=sz[:], in_=zb[c, h][:].rearrange("p t n -> p n t"))
+            sy = ring.tile([P, TC, 4], BF16, name="sy", align_bytes=64)
+            nc.vector.tensor_copy(out=sy[:], in_=yb[c, h][:].rearrange("p t n -> p n t"))
+            quantize(2, c, 2 + h, sz)
+            quantize(2, c, h, sy)
+
+        y_half = sb("y_half", [P, 4, D], BF16)
+
+        def turn(c, h, i):
+            toks = slice(P * i, P * i + P)
+            ty = psum.tile([P, 4, P], F32, name="mb", bufs=4)
+            for t in range(4):
+                nc.tensor.transpose(ty[:, t, :], y1[c, h][:, t, toks], ident[:])
+            tz = psum.tile([P, 4, P], F32, name="tp", bufs=2)
+            for t in range(4):
+                nc.tensor.matmul(tz[:, t, :], lhsT=z1[c, h][:, t, toks], rhs=ident[:], is_transpose=True, start=True, stop=False)
+                nc.tensor.matmul(tz[:, t, :], lhsT=t2[c, h][:, t, toks], rhs=ident[:], is_transpose=True, start=False, stop=True)
+            return ty, tz
+
+        def finish(c, h, i, ty, tz):
+            it = TT * c + i
+            cols = slice(512 * h, 512 * h + 512)
+            z2 = ring.tile([P, 512], F32, name="z2", bufs=3)
+            y2 = ring.tile([P, 512], F32, name="y2", bufs=3)
+            nc.vector.scalar_tensor_tensor(
+                out=z2[:].rearrange("p (m t) -> p m t", t=4), in0=tz[:].rearrange("p t m -> p m t"), scalar=0.5,
+                in1=y_half[:, it, cols].rearrange("p (m t) -> p m t", t=4), op0=ALU.mult, op1=ALU.subtract,
+            )
+            nc.vector.scalar_tensor_tensor(
+                out=y2[:].rearrange("p (m t) -> p m t", t=4), in0=z2[:].rearrange("p (m t) -> p m t", t=4), scalar=0.5,
+                in1=ty[:].rearrange("p t m -> p m t"), op0=ALU.mult, op1=ALU.add,
+            )
+            rows = slice(P * it, P * it + P)
+            nc.sync.dma_start(out=out_1[rows, cols], in_=z2[:])
+            nc.sync.dma_start(out=out_0[rows, cols], in_=y2[:])
+
+        def half_y(i):
+            nc.scalar.mul(y_half[:, i, :], y_nat[:, i, :], 0.5)
+
+        with tc.manual_schedule():
+            transpose_in(0, (0, 1))
+            permute_w(0, (0, 1))
+            gain_and_quantize(0, (0, 1))
+            small_casts()
+            widen_u(0)
+            widen_u(1)
+            transpose_in(0, (2, 3))
+            gain_and_quantize(0, (2, 3))
+            permute_scales(0)
+            permute_w(0, (2, 3))
+            make_u(0)
+            drift(0, 0)
+            widen_u(2)
+            widen_u(3)
+            permute_scales(1)
+            permute_v(0)
+            make_u(1)
+            drift(0, 1)
+            half_y(0)
+            matmuls(1, 0, 0)
+            permute_w(1, (0, 1, 2, 3))
+            permute_v(1)
+            transpose_in(1, (0, 1, 2, 3))
+            state(0, 0)
+            matmuls(1, 0, 1)
+            gain_and_quantize(1, (0, 1, 2, 3))
+            second_operand(0, 0)
+            matmuls(1, 1, 0)
+            drift(1, 0)
+            state(0, 1)
+            matmuls(1, 1, 1)
+            drift(1, 1)
+            state(1, 0)
+            second_operand(0, 1)
+            matmuls(2, 0, 0, early=True)
+            state(1, 1)
+            second_operand(1, 0)
+            matmuls(2, 0, 1)
+            units = [(0, 0, 0), (0, 0, 1), (0, 1, 0), (0, 1, 1), (1, 0, 0), (1, 0, 1), (1, 1, 0), (1, 1, 1)]
+            turned = {}
+            for n in range(3):
+                turned[n] = turn(*units[n])
+            half_y(1)
+            second_operand(1, 1)
+            finish(*units[0], *turned[0])
+            matmuls(2, 1, 0, early=True)
+            half_y(2)
+            half_y(3)
+            for n in (1, 2):
+                finish(*units[n], *turned[n])
+            turned[3] = turn(*units[3])
+            finish(*units[3], *turned[3])
+            matmuls(2, 1, 1)
+            for n in range(4, 8):
+                turned[n] = turn(*units[n])
+                finish(*units[n], *turned[n])

@@ -103,16 +103,17 @@ def tile_coupledoscillatorrnntwosubsteps_d1p_kernel(
             nc.vector.tensor_copy(out=bf[:], in_=bb[:].rearrange("p q t -> p (q t)"))
 
         def gain(q):
-            return gb[:, q, :].unsqueeze(1).to_broadcast([P, TC, 4])
+            return gb[:, q, :].rearrange("p (u e) -> p u e", e=2).unsqueeze(1).to_broadcast([P, TC, 2, 2])
 
         wp = sb("wp", [P, 4, D], I32)
         vp = sb("vp", [P, D], I32)
         scp = sb("scp", [P, 2, D], U8)
 
-        def permute_scales(x):
+        def permute_scales(x, h):
+            cols = slice(512 * h, 512 * h + 512)
             nc.vector.tensor_copy(
-                out=scp[:, x, :].rearrange("p (h t m) -> p h t m", h=2, t=4),
-                in_=sc_raw[:, x, :].rearrange("p (h m t) -> p h t m", h=2, t=4),
+                out=scp[:, x, cols].rearrange("p (t m) -> p t m", t=4),
+                in_=sc_raw[:, x, cols].rearrange("p (m t) -> p t m", t=4),
             )
 
         def permute_w(h, qs):
@@ -141,25 +142,30 @@ def tile_coupledoscillatorrnntwosubsteps_d1p_kernel(
                     scale=us[:, i, j : j + 1],
                 )
 
-        def words_transposed(dst, nat, c, q, copy=nc.scalar.copy):
+        def words_transposed(nat, c, q):
             bank = psum.tile([P, TT, 2, P], F32, name="tp", bufs=2)
             for i in range(TT):
                 words = nat[:, TT * c + i, :].bitcast(F32)
                 for e in range(2):
                     nc.tensor.transpose(bank[:, i, e, :], words[:, 256 * q + e : 256 * (q + 1) : 2], ident[:])
-            copy(
-                out=dst.rearrange("p (i r) t -> p i (r t)", i=TT).bitcast(F32).rearrange("p i (r e) -> p i r e", e=2),
-                in_=bank[:].rearrange("p i e r -> p i r e"),
-            )
+            return bank
 
         u_q = sb("u_q", [P, CHUNKS, TC], I32)
         u_s = sb("u_s", [P, CHUNKS, TC], U8)
 
-        def make_u(c):
-            ut = ring.tile([P, TC, 4], BF16, name="ut", align_bytes=64)
-            words_transposed(ut[:], u_wide, c, 0)
+        u_turned = {}
+
+        def turn_u(c):
+            ut = u_turned[c] = ring.tile([P, TC, 4], BF16, name="ut", align_bytes=64)
+            bank = words_transposed(u_wide, c, 0)
+            nc.scalar.copy(
+                out=ut[:].rearrange("p (i r) t -> p i (r t)", i=TT).bitcast(F32).rearrange("p i (r e) -> p i r e", e=2),
+                in_=bank[:].rearrange("p i e r -> p i r e"),
+            )
+
+        def quantize_u(c):
             nc.vector.quantize_mx(
-                out=u_q[:, c, :].bitcast(FP8X4), scales=u_s[:, c, :], in_=ut[:].rearrange("p n t -> p (n t)")
+                out=u_q[:, c, :].bitcast(FP8X4), scales=u_s[:, c, :], in_=u_turned[c][:].rearrange("p n t -> p (n t)")
             )
 
         raw = {}
@@ -178,14 +184,21 @@ def tile_coupledoscillatorrnntwosubsteps_d1p_kernel(
         def transpose_in(c, qs):
             for q in qs:
                 nat = y_nat if q < 2 else z_nat
-                raw[c, q] = sb("raw%d%d" % (c, q), [P, TC, 4], BF16)
-                words_transposed(raw[c, q][:], nat, c, q % 2, copy=nc.vector.tensor_copy if (c == 0 and q == 3) else nc.scalar.copy)
+                raw[c, q] = sb("raw%d%d" % (c, q), [P, 2, TC, 2], BF16)
+                bank = words_transposed(nat, c, q % 2)
+                nc.scalar.copy(
+                    out=raw[c, q][:].rearrange("p u n e -> p u (n e)").bitcast(F32).rearrange("p u (i r) -> p i u r", i=TT),
+                    in_=bank[:],
+                )
 
         def gain_and_quantize(c, qs):
             tiles = []
             for q in qs:
                 s = ring.tile([P, TC, 4], BF16, name="s1", bufs=4, align_bytes=64)
-                nc.vector.tensor_tensor(out=s[:], in0=raw[c, q][:], in1=gain(q), op=ALU.mult)
+                nc.vector.tensor_tensor(
+                    out=s[:].rearrange("p n (u e) -> p n u e", e=2), in0=raw[c, q][:].rearrange("p u n e -> p n u e"),
+                    in1=gain(q), op=ALU.mult,
+                )
                 tiles.append(s)
             for q, s in zip(qs, tiles):
                 quantize(1, c, q, s)
@@ -233,9 +246,8 @@ def tile_coupledoscillatorrnntwosubsteps_d1p_kernel(
             for i in range(2):
                 m = mb[c, h, i] = psum.tile([P, 2, TC], F32, name="mb", bufs=4)
                 for e in range(2):
-                    t = 2 * i + e
-                    nc.tensor.matmul(m[:, e, :], lhsT=eye75[:], rhs=raw[c, 2 + h][:, :, t], start=True, stop=False)
-                    nc.tensor.matmul(m[:, e, :], lhsT=eyem5[:], rhs=raw[c, h][:, :, t], start=False, stop=True)
+                    nc.tensor.matmul(m[:, e, :], lhsT=eye75[:], rhs=raw[c, 2 + h][:, i, :, e], start=True, stop=False)
+                    nc.tensor.matmul(m[:, e, :], lhsT=eyem5[:], rhs=raw[c, h][:, i, :, e], start=False, stop=True)
 
         def state(c, h):
             z = z1[c, h] = sb("z1_%d%d" % (c, h), [P, 4, TC], F32)
@@ -253,79 +265,107 @@ def tile_coupledoscillatorrnntwosubsteps_d1p_kernel(
                 pair = slice(2 * i, 2 * i + 2)
                 nc.vector.scalar_tensor_tensor(
                     out=y[:, pair, :], in0=z[:, pair, :], scalar=0.5,
-                    in1=raw[c, h][:].rearrange("p n t -> p t n")[:, pair, :], op0=ALU.mult, op1=ALU.add,
+                    in1=raw[c, h][:, i].rearrange("p n e -> p e n"), op0=ALU.mult, op1=ALU.add,
                 )
-            for t in range(4):
-                nc.scalar.activation(out=yb[c, h][:, t, :], in_=y[:, t, :], func=ACT.Copy, scale=gf[:, h, t : t + 1])
+            if (c, h) != (1, 1):
+                for t in range(4):
+                    nc.scalar.activation(out=yb[c, h][:, t, :], in_=y[:, t, :], func=ACT.Copy, scale=gf[:, h, t : t + 1])
 
         def second_operand(c, h):
-            sz = ring.tile([P, TC, 4], BF16, name="sz", align_bytes=64)
-            nc.vector.tensor_copy(out=sz[:], in_=zb[c, h][:].rearrange("p t n -> p n t"))
             sy = ring.tile([P, TC, 4], BF16, name="sy", align_bytes=64)
-            nc.vector.tensor_copy(out=sy[:], in_=yb[c, h][:].rearrange("p t n -> p n t"))
+            sz = ring.tile([P, TC, 4], BF16, name="sz", align_bytes=64)
+            if (c, h) == (1, 1):
+                nc.vector.tensor_tensor(
+                    out=sy[:], in0=y1[c, h][:].rearrange("p t n -> p n t"),
+                    in1=gb[:, h, :].unsqueeze(1).to_broadcast([P, TC, 4]), op=ALU.mult,
+                )
+            nc.vector.tensor_copy(out=sz[:], in_=zb[c, h][:].rearrange("p t n -> p n t"))
+            if (c, h) != (1, 1):
+                nc.vector.tensor_copy(out=sy[:], in_=yb[c, h][:].rearrange("p t n -> p n t"))
             quantize(2, c, 2 + h, sz)
             quantize(2, c, h, sy)
 
         y_half = sb("y_half", [P, 4, D], BF16)
 
-        def turn(c, h, i):
+        def turn_y(n):
+            c, h, i = units[n]
             toks = slice(P * i, P * i + P)
-            ty = psum.tile([P, 4, P], F32, name="mb", bufs=4)
+            ty = turned_y[n] = psum.tile([P, 4, P], F32, name="mb", bufs=4)
             for t in range(4):
                 nc.tensor.transpose(ty[:, t, :], y1[c, h][:, t, toks], ident[:])
-            tz = psum.tile([P, 4, P], F32, name="tp", bufs=2)
+
+        def turn_z(n):
+            c, h, i = units[n]
+            toks = slice(P * i, P * i + P)
+            tz = turned_z[n] = psum.tile([P, 4, P], F32, name="tp", bufs=2)
             for t in range(4):
                 nc.tensor.matmul(tz[:, t, :], lhsT=z1[c, h][:, t, toks], rhs=ident[:], is_transpose=True, start=True, stop=False)
                 nc.tensor.matmul(tz[:, t, :], lhsT=t2[c, h][:, t, toks], rhs=ident[:], is_transpose=True, start=False, stop=True)
-            return ty, tz
 
-        def finish(c, h, i, ty, tz):
-            it = TT * c + i
+        z2 = {}
+
+        def finish_z(n):
+            c, h, i = units[n]
             cols = slice(512 * h, 512 * h + 512)
-            z2 = ring.tile([P, 512], F32, name="z2", bufs=3)
-            y2 = ring.tile([P, 512], F32, name="y2", bufs=3)
+            rows = slice(TC * c + P * i, TC * c + P * i + P)
+            z2[n] = ring.tile([P, 512], F32, name="z2", bufs=4)
             nc.vector.scalar_tensor_tensor(
-                out=z2[:].rearrange("p (m t) -> p m t", t=4), in0=tz[:].rearrange("p t m -> p m t"), scalar=0.5,
-                in1=y_half[:, it, cols].rearrange("p (m t) -> p m t", t=4), op0=ALU.mult, op1=ALU.subtract,
+                out=z2[n][:].rearrange("p (m t) -> p m t", t=4), in0=turned_z[n][:].rearrange("p t m -> p m t"), scalar=0.5,
+                in1=y_half[:, TT * c + i, cols].rearrange("p (m t) -> p m t", t=4), op0=ALU.mult, op1=ALU.subtract,
             )
+            nc.sync.dma_start(out=out_1[rows, cols], in_=z2[n][:])
+
+        def finish_y(n):
+            c, h, i = units[n]
+            cols = slice(512 * h, 512 * h + 512)
+            rows = slice(TC * c + P * i, TC * c + P * i + P)
+            y2 = ring.tile([P, 512], F32, name="y2", bufs=4)
             nc.vector.scalar_tensor_tensor(
-                out=y2[:].rearrange("p (m t) -> p m t", t=4), in0=z2[:].rearrange("p (m t) -> p m t", t=4), scalar=0.5,
-                in1=ty[:].rearrange("p t m -> p m t"), op0=ALU.mult, op1=ALU.add,
+                out=y2[:].rearrange("p (m t) -> p m t", t=4), in0=z2[n][:].rearrange("p (m t) -> p m t", t=4), scalar=0.5,
+                in1=turned_y[n][:].rearrange("p t m -> p m t"), op0=ALU.mult, op1=ALU.add,
             )
-            rows = slice(P * it, P * it + P)
-            nc.sync.dma_start(out=out_1[rows, cols], in_=z2[:])
             nc.sync.dma_start(out=out_0[rows, cols], in_=y2[:])
 
+        units = [(c, h, i) for c in range(CHUNKS) for h in range(2) for i in range(TT)]
+        turned_y = {}
+        turned_z = {}
+
         def half_y(i):
-            nc.scalar.mul(y_half[:, i, :], y_nat[:, i, :], 0.5)
+            nc.vector.tensor_scalar(
+                out=y_half[:, i : i + 2, :], in0=y_nat[:, i : i + 2, :], scalar1=0.5, scalar2=None, op0=ALU.mult
+            )
 
         with tc.manual_schedule():
             transpose_in(0, (0, 1))
+            half_y(0)
             permute_w(0, (0, 1))
             gain_and_quantize(0, (0, 1))
             small_casts()
             widen_u(0)
             widen_u(1)
             transpose_in(0, (2, 3))
-            gain_and_quantize(0, (2, 3))
-            permute_scales(0)
             permute_w(0, (2, 3))
-            make_u(0)
+            gain_and_quantize(0, (2, 3))
+            turn_u(0)
+            permute_scales(0, 0)
+            quantize_u(0)
             drift(0, 0)
             widen_u(2)
             widen_u(3)
-            permute_scales(1)
+            permute_scales(1, 0)
             permute_v(0)
-            make_u(1)
-            drift(0, 1)
-            half_y(0)
             matmuls(1, 0, 0)
+            permute_scales(0, 1)
+            permute_scales(1, 1)
             permute_w(1, (0, 1, 2, 3))
             permute_v(1)
             transpose_in(1, (0, 1, 2, 3))
+            turn_u(1)
+            drift(0, 1)
             state(0, 0)
             matmuls(1, 0, 1)
             gain_and_quantize(1, (0, 1, 2, 3))
+            quantize_u(1)
             second_operand(0, 0)
             matmuls(1, 1, 0)
             drift(1, 0)
@@ -338,21 +378,26 @@ def tile_coupledoscillatorrnntwosubsteps_d1p_kernel(
             state(1, 1)
             second_operand(1, 0)
             matmuls(2, 0, 1)
-            units = [(0, 0, 0), (0, 0, 1), (0, 1, 0), (0, 1, 1), (1, 0, 0), (1, 0, 1), (1, 1, 0), (1, 1, 1)]
-            turned = {}
-            for n in range(3):
-                turned[n] = turn(*units[n])
-            half_y(1)
+            for n in (0, 1):
+                turn_y(n)
+                turn_z(n)
             second_operand(1, 1)
-            finish(*units[0], *turned[0])
+            finish_z(0)
+            finish_z(1)
+            finish_y(0)
+            finish_y(1)
             matmuls(2, 1, 0, early=True)
             half_y(2)
-            half_y(3)
-            for n in (1, 2):
-                finish(*units[n], *turned[n])
-            turned[3] = turn(*units[3])
-            finish(*units[3], *turned[3])
+            for n in (2, 3):
+                turn_y(n)
+                turn_z(n)
+            finish_z(2)
+            finish_z(3)
+            finish_y(2)
+            finish_y(3)
             matmuls(2, 1, 1)
             for n in range(4, 8):
-                turned[n] = turn(*units[n])
-                finish(*units[n], *turned[n])
+                turn_y(n)
+                turn_z(n)
+                finish_z(n)
+                finish_y(n)

@@ -45,7 +45,6 @@ def tile_coupledoscillatorrnntwosubsteps_d1p_kernel(
         gb = sb("gb", [P, 4, 4], BF16)
         nc.scalar.dma_start(out=gb[:], in_=g.rearrange("(q p t) -> p q t", p=P, t=4))
         bb = sb("bb", [P, 2, 4], BF16)
-        nc.scalar.dma_start(out=bb[:], in_=b.rearrange("(q p t) -> p q t", p=P, t=4))
 
         w_raw = sb("w_raw", [P, 4, D], I32)
         v_raw = sb("v_raw", [P, D], I32)
@@ -57,36 +56,36 @@ def tile_coupledoscillatorrnntwosubsteps_d1p_kernel(
         z_nat = sb("z_nat", [P, 4, D], BF16)
         u_raw = sb("u_raw", [P, 4, E], U8)
 
-        def load_w(h, q):
+        def load_w(h, qs=slice(0, 4)):
             nc.sync.dma_start(
-                out=w_raw[:, q : q + 2, 512 * h : 512 * h + 512],
-                in_=w_view[:, q : q + 2, 2048 * h : 2048 * h + 2048].bitcast(I32),
+                out=w_raw[:, qs, 512 * h : 512 * h + 512], in_=w_view[:, qs, 2048 * h : 2048 * h + 2048].bitcast(I32)
             )
 
-        def load_v(h):
+        def load_w_scales(q):
             nc.sync.dma_start(
-                out=v_raw[:, 512 * h : 512 * h + 512], in_=v_view[:, 2048 * h : 2048 * h + 2048].bitcast(I32)
+                out=sc_raw[32 * q : 32 * q + 16, 0, :].bitcast(I32), in_=w_scales[:, 4 * q : 4 * q + 4, :].bitcast(I32)
+            )
+
+        def load_v_scales(q):
+            nc.sync.dma_start(
+                out=sc_raw[32 * q : 32 * q + 4, 1, :].bitcast(I32), in_=v_scales[0, 4 * q : 4 * q + 4, :].bitcast(I32)
             )
 
         nc.sync.dma_start(out=y_nat[:, 0:2, :], in_=y_view[:, 0:2, :])
-        load_w(0, 0)
         nc.sync.dma_start(out=u_raw[:], in_=u_bytes.rearrange("(i p) k -> p i k", p=P))
         nc.sync.dma_start(out=z_nat[:, 0:2, :], in_=z_view[:, 0:2, :])
-        load_w(0, 2)
-        load_v(0)
-        for q in range(4):
-            nc.sync.dma_start(
-                out=sc_raw[32 * q : 32 * q + 16, 0, :].bitcast(I32),
-                in_=w_scales[:, 4 * q : 4 * q + 4, :].bitcast(I32),
-            )
-        for q in range(4):
-            nc.gpsimd.dma_start(
-                out=sc_raw[32 * q : 32 * q + 4, 1, :].bitcast(I32),
-                in_=v_scales[0, 4 * q : 4 * q + 4, :].bitcast(I32),
-            )
-        load_w(1, 0)
-        load_w(1, 2)
-        load_v(1)
+        load_w_scales(0)
+        load_w_scales(1)
+        load_w(0)
+        load_w_scales(2)
+        load_w_scales(3)
+        load_v_scales(0)
+        load_v_scales(1)
+        load_v_scales(2)
+        load_v_scales(3)
+        nc.sync.dma_start(out=v_raw[:], in_=v_view.bitcast(I32))
+        nc.sync.dma_start(out=bb[:], in_=b.rearrange("(q p t) -> p q t", p=P, t=4))
+        load_w(1)
         nc.sync.dma_start(out=y_nat[:, 2:4, :], in_=y_view[:, 2:4, :])
         nc.sync.dma_start(out=z_nat[:, 2:4, :], in_=z_view[:, 2:4, :])
 
@@ -98,8 +97,10 @@ def tile_coupledoscillatorrnntwosubsteps_d1p_kernel(
         gf = sb("gf", [P, 4, 4], F32)
         bf = sb("bf", [P, 8], F32)
 
-        def small_casts():
+        def cast_gain():
             nc.vector.tensor_copy(out=gf[:], in_=gb[:])
+
+        def cast_bias():
             nc.vector.tensor_copy(out=bf[:], in_=bb[:].rearrange("p q t -> p (q t)"))
 
         def gain(q):
@@ -109,26 +110,24 @@ def tile_coupledoscillatorrnntwosubsteps_d1p_kernel(
         vp = sb("vp", [P, D], I32)
         scp = sb("scp", [P, 2, D], U8)
 
-        def permute_scales(x, h):
+        def permute_w(h, qs=slice(0, 4)):
             cols = slice(512 * h, 512 * h + 512)
             nc.vector.tensor_copy(
-                out=scp[:, x, cols].rearrange("p (t m) -> p t m", t=4),
-                in_=sc_raw[:, x, cols].rearrange("p (m t) -> p t m", t=4),
+                out=wp[:, qs, cols].rearrange("p q (t m) -> p q m t", t=4),
+                in_=w_raw[:, qs, cols].rearrange("p q (m t) -> p q m t", t=4),
             )
 
-        def permute_w(h, qs):
+        def permute_scales(h):
             cols = slice(512 * h, 512 * h + 512)
-            for q in qs:
-                nc.vector.tensor_copy(
-                    out=wp[:, q, cols].rearrange("p (t m) -> p t m", t=4),
-                    in_=w_raw[:, q, cols].rearrange("p (m t) -> p t m", t=4),
-                )
+            nc.vector.tensor_copy(
+                out=scp[:, :, cols].rearrange("p x (t m) -> p x m t", t=4),
+                in_=sc_raw[:, :, cols].rearrange("p x (m t) -> p x m t", t=4),
+            )
 
         def permute_v(h):
             cols = slice(512 * h, 512 * h + 512)
             nc.vector.tensor_copy(
-                out=vp[:, cols].rearrange("p (t m) -> p t m", t=4),
-                in_=v_raw[:, cols].rearrange("p (m t) -> p t m", t=4),
+                out=vp[:, cols].rearrange("p (t m) -> p m t", t=4), in_=v_raw[:, cols].rearrange("p (m t) -> p m t", t=4)
             )
 
         u_wide = sb("u_wide", [P, 4, E], BF16)
@@ -217,6 +216,7 @@ def tile_coupledoscillatorrnntwosubsteps_d1p_kernel(
                     start=(q == order[0]), stop=(q == order[-1]),
                 )
 
+        made = {}
         t1 = {}
         z1 = {}
         y1 = {}
@@ -225,16 +225,19 @@ def tile_coupledoscillatorrnntwosubsteps_d1p_kernel(
         yb = {}
         mb = {}
 
-        def matmuls(k, c, h, early=False):
-            if k == 1:
+        def matmuls(k, c, h, early=False, pairs=(0, 1)):
+            if (k, c, h) in made:
+                t = made[k, c, h]
+            elif k == 1:
                 t = t1[c, h] = ring.tile([P, 4, TC], F32, name="t1", bufs=4)
             else:
                 t = t2[c, h] = sb("t2_%d%d" % (c, h), [P, 4, TC], F32)
-            banks = [psum.tile([P, 2, TC], F32, name="mx", bufs=2) for i in range(2)]
+            made[k, c, h] = t
+            banks = {i: psum.tile([P, 2, TC], F32, name="mx", bufs=2) for i in pairs}
             if early:
                 for i in range(2):
                     mx_passes(banks[i][:, 0, :], 4 * h + 2 * i, k, c, ORDER[k][:3])
-            for i in range(2):
+            for i in pairs:
                 bank = banks[i]
                 for e in range(2):
                     mx_passes(bank[:, e, :], 4 * h + 2 * i + e, k, c, ORDER[k][3:] if early and e == 0 else ORDER[k])
@@ -267,21 +270,14 @@ def tile_coupledoscillatorrnntwosubsteps_d1p_kernel(
                     out=y[:, pair, :], in0=z[:, pair, :], scalar=0.5,
                     in1=raw[c, h][:, i].rearrange("p n e -> p e n"), op0=ALU.mult, op1=ALU.add,
                 )
-            if (c, h) != (1, 1):
-                for t in range(4):
-                    nc.scalar.activation(out=yb[c, h][:, t, :], in_=y[:, t, :], func=ACT.Copy, scale=gf[:, h, t : t + 1])
+            for t in range(4):
+                nc.scalar.activation(out=yb[c, h][:, t, :], in_=y[:, t, :], func=ACT.Copy, scale=gf[:, h, t : t + 1])
 
         def second_operand(c, h):
             sy = ring.tile([P, TC, 4], BF16, name="sy", align_bytes=64)
             sz = ring.tile([P, TC, 4], BF16, name="sz", align_bytes=64)
-            if (c, h) == (1, 1):
-                nc.vector.tensor_tensor(
-                    out=sy[:], in0=y1[c, h][:].rearrange("p t n -> p n t"),
-                    in1=gb[:, h, :].unsqueeze(1).to_broadcast([P, TC, 4]), op=ALU.mult,
-                )
             nc.vector.tensor_copy(out=sz[:], in_=zb[c, h][:].rearrange("p t n -> p n t"))
-            if (c, h) != (1, 1):
-                nc.vector.tensor_copy(out=sy[:], in_=yb[c, h][:].rearrange("p t n -> p n t"))
+            nc.vector.tensor_copy(out=sy[:], in_=yb[c, h][:].rearrange("p t n -> p n t"))
             quantize(2, c, 2 + h, sz)
             quantize(2, c, h, sy)
 
@@ -337,31 +333,29 @@ def tile_coupledoscillatorrnntwosubsteps_d1p_kernel(
 
         with tc.manual_schedule():
             transpose_in(0, (0, 1))
-            half_y(0)
-            permute_w(0, (0, 1))
+            cast_gain()
             gain_and_quantize(0, (0, 1))
-            small_casts()
             widen_u(0)
             widen_u(1)
             transpose_in(0, (2, 3))
-            permute_w(0, (2, 3))
+            half_y(0)
             gain_and_quantize(0, (2, 3))
             turn_u(0)
-            permute_scales(0, 0)
             quantize_u(0)
             drift(0, 0)
             widen_u(2)
             widen_u(3)
-            permute_scales(1, 0)
+            permute_w(0)
+            permute_scales(0)
             permute_v(0)
-            matmuls(1, 0, 0)
-            permute_scales(0, 1)
-            permute_scales(1, 1)
-            permute_w(1, (0, 1, 2, 3))
-            permute_v(1)
-            transpose_in(1, (0, 1, 2, 3))
+            cast_bias()
             turn_u(1)
             drift(0, 1)
+            matmuls(1, 0, 0)
+            permute_w(1)
+            permute_scales(1)
+            permute_v(1)
+            transpose_in(1, (0, 1, 2, 3))
             state(0, 0)
             matmuls(1, 0, 1)
             gain_and_quantize(1, (0, 1, 2, 3))

@@ -40,25 +40,28 @@ def tile_coupledoscillatorrnntwosubsteps_d1p_kernel(
         ident = sb("ident", [P, P], F32)
         make_identity(nc, ident[:])
 
-        us = sb("us", [P, 4, 4], F32)
-        nc.scalar.dma_start(out=us[:], in_=u_scale.rearrange("(i p) j -> p i j", p=P))
         gb = sb("gb", [P, 4, 4], BF16)
         nc.scalar.dma_start(out=gb[:], in_=g.rearrange("(q p t) -> p q t", p=P, t=4))
+        us = sb("us", [P, 4, 4], F32)
+        nc.scalar.dma_start(out=us[:], in_=u_scale.rearrange("(i p) j -> p i j", p=P))
         bb = sb("bb", [P, 2, 4], BF16)
 
-        w_raw = sb("w_raw", [P, 4, D], I32)
+        w_raw = [sb("w_raw%d" % h, [P, 4, 512], I32) for h in range(2)]
         v_raw = sb("v_raw", [P, D], I32)
         w_view = w_words.rearrange("q p n t -> p q (n t)")
         v_view = v_words[0].rearrange("p n t -> p (n t)")
-        y_view = y0.rearrange("(i p) d -> p i d", p=P)
-        z_view = z0.rearrange("(i p) d -> p i d", p=P)
-        y_nat = sb("y_nat", [P, 4, D], BF16)
-        z_nat = sb("z_nat", [P, 4, D], BF16)
+        y_view = y0.rearrange("(c i p) d -> p c i d", i=TT, p=P)
+        z_view = z0.rearrange("(c i p) d -> p c i d", i=TT, p=P)
+        y_nat = {(c, q): sb("y_nat%d%d" % (c, q), [P, TT, 512], BF16) for c in range(CHUNKS) for q in range(2)}
+        z_nat = {(c, q): sb("z_nat%d%d" % (c, q), [P, TT, 512], BF16) for c in range(CHUNKS) for q in range(2)}
+
+        def load_state(nat, view, c, q):
+            nc.sync.dma_start(out=nat[c, q][:], in_=view[:, c, :, 512 * q : 512 * q + 512])
         u_raw = sb("u_raw", [P, 4, E], U8)
 
         def load_w(h, qs=slice(0, 4)):
             nc.sync.dma_start(
-                out=w_raw[:, qs, 512 * h : 512 * h + 512], in_=w_view[:, qs, 2048 * h : 2048 * h + 2048].bitcast(I32)
+                out=w_raw[h][:, qs, :], in_=w_view[:, qs, 2048 * h : 2048 * h + 2048].bitcast(I32)
             )
 
         def load_w_scales(q):
@@ -71,14 +74,16 @@ def tile_coupledoscillatorrnntwosubsteps_d1p_kernel(
                 out=sc_raw[32 * q : 32 * q + 4, 1, :].bitcast(I32), in_=v_scales[0, 4 * q : 4 * q + 4, :].bitcast(I32)
             )
 
-        nc.sync.dma_start(out=y_nat[:, 0:2, :], in_=y_view[:, 0:2, :])
-        nc.sync.dma_start(out=u_raw[:], in_=u_bytes.rearrange("(i p) k -> p i k", p=P))
-        nc.sync.dma_start(out=z_nat[:, 0:2, :], in_=z_view[:, 0:2, :])
+        load_state(y_nat, y_view, 0, 0)
+        load_state(y_nat, y_view, 0, 1)
+        load_state(z_nat, z_view, 0, 0)
+        load_state(z_nat, z_view, 0, 1)
         load_w_scales(0)
         load_w_scales(1)
-        load_w(0)
         load_w_scales(2)
         load_w_scales(3)
+        nc.sync.dma_start(out=u_raw[:], in_=u_bytes.rearrange("(i p) k -> p i k", p=P))
+        load_w(0)
         load_v_scales(0)
         load_v_scales(1)
         load_v_scales(2)
@@ -86,19 +91,22 @@ def tile_coupledoscillatorrnntwosubsteps_d1p_kernel(
         nc.sync.dma_start(out=v_raw[:], in_=v_view.bitcast(I32))
         nc.sync.dma_start(out=bb[:], in_=b.rearrange("(q p t) -> p q t", p=P, t=4))
         load_w(1)
-        nc.sync.dma_start(out=y_nat[:, 2:4, :], in_=y_view[:, 2:4, :])
-        nc.sync.dma_start(out=z_nat[:, 2:4, :], in_=z_view[:, 2:4, :])
+        load_state(y_nat, y_view, 1, 0)
+        load_state(y_nat, y_view, 1, 1)
+        load_state(z_nat, z_view, 1, 0)
+        load_state(z_nat, z_view, 1, 1)
 
-        eye75 = sb("eye75", [P, P], BF16)
-        nc.vector.tensor_scalar(out=eye75[:], in0=ident[:], scalar1=0.75, scalar2=None, op0=ALU.mult)
-        eyem5 = sb("eyem5", [P, P], BF16)
-        nc.vector.tensor_scalar(out=eyem5[:], in0=ident[:], scalar1=-0.5, scalar2=None, op0=ALU.mult)
+        eye_z = sb("eye_z", [P, P], BF16)
+        nc.vector.tensor_scalar(out=eye_z[:], in0=ident[:], scalar1=0.375, scalar2=None, op0=ALU.mult)
+        eye_y = sb("eye_y", [P, P], BF16)
+        nc.vector.tensor_scalar(out=eye_y[:], in0=ident[:], scalar1=-0.25, scalar2=None, op0=ALU.mult)
 
         gf = sb("gf", [P, 4, 4], F32)
         bf = sb("bf", [P, 8], F32)
 
         def cast_gain():
-            nc.vector.tensor_copy(out=gf[:], in_=gb[:])
+            nc.vector.tensor_copy(out=gf[:, 0:2, :], in_=gb[:, 0:2, :])
+            nc.vector.tensor_scalar(out=gf[:, 2:4, :], in0=gb[:, 2:4, :], scalar1=2.0, scalar2=None, op0=ALU.mult)
 
         def cast_bias():
             nc.vector.tensor_copy(out=bf[:], in_=bb[:].rearrange("p q t -> p (q t)"))
@@ -106,22 +114,21 @@ def tile_coupledoscillatorrnntwosubsteps_d1p_kernel(
         def gain(q):
             return gb[:, q, :].rearrange("p (u e) -> p u e", e=2).unsqueeze(1).to_broadcast([P, TC, 2, 2])
 
-        wp = sb("wp", [P, 4, D], I32)
+        wp = [sb("wp%d" % h, [P, 4, 512], I32) for h in range(2)]
         vp = sb("vp", [P, D], I32)
         scp = sb("scp", [P, 2, D], U8)
 
         def permute_w(h, qs=slice(0, 4)):
-            cols = slice(512 * h, 512 * h + 512)
             nc.vector.tensor_copy(
-                out=wp[:, qs, cols].rearrange("p q (t m) -> p q m t", t=4),
-                in_=w_raw[:, qs, cols].rearrange("p q (m t) -> p q m t", t=4),
+                out=wp[h][:, qs, :].rearrange("p q (t m) -> p q m t", t=4),
+                in_=w_raw[h][:, qs, :].rearrange("p q (m t) -> p q m t", t=4),
             )
 
-        def permute_scales(h):
+        def permute_scales(x, h):
             cols = slice(512 * h, 512 * h + 512)
             nc.vector.tensor_copy(
-                out=scp[:, :, cols].rearrange("p x (t m) -> p x m t", t=4),
-                in_=sc_raw[:, :, cols].rearrange("p x (m t) -> p x m t", t=4),
+                out=scp[:, x, cols].rearrange("p (t m) -> p m t", t=4),
+                in_=sc_raw[:, x, cols].rearrange("p (m t) -> p m t", t=4),
             )
 
         def permute_v(h):
@@ -141,12 +148,12 @@ def tile_coupledoscillatorrnntwosubsteps_d1p_kernel(
                     scale=us[:, i, j : j + 1],
                 )
 
-        def words_transposed(nat, c, q):
+        def words_transposed(nat):
             bank = psum.tile([P, TT, 2, P], F32, name="tp", bufs=2)
             for i in range(TT):
-                words = nat[:, TT * c + i, :].bitcast(F32)
+                words = nat[:, i, :].bitcast(F32)
                 for e in range(2):
-                    nc.tensor.transpose(bank[:, i, e, :], words[:, 256 * q + e : 256 * (q + 1) : 2], ident[:])
+                    nc.tensor.transpose(bank[:, i, e, :], words[:, e::2], ident[:])
             return bank
 
         u_q = sb("u_q", [P, CHUNKS, TC], I32)
@@ -156,7 +163,7 @@ def tile_coupledoscillatorrnntwosubsteps_d1p_kernel(
 
         def turn_u(c):
             ut = u_turned[c] = ring.tile([P, TC, 4], BF16, name="ut", align_bytes=64)
-            bank = words_transposed(u_wide, c, 0)
+            bank = words_transposed(u_wide[:, TT * c : TT * c + TT, :])
             nc.scalar.copy(
                 out=ut[:].rearrange("p (i r) t -> p i (r t)", i=TT).bitcast(F32).rearrange("p i (r e) -> p i r e", e=2),
                 in_=bank[:].rearrange("p i e r -> p i r e"),
@@ -184,7 +191,7 @@ def tile_coupledoscillatorrnntwosubsteps_d1p_kernel(
             for q in qs:
                 nat = y_nat if q < 2 else z_nat
                 raw[c, q] = sb("raw%d%d" % (c, q), [P, 2, TC, 2], BF16)
-                bank = words_transposed(nat, c, q % 2)
+                bank = words_transposed(nat[c, q % 2])
                 nc.scalar.copy(
                     out=raw[c, q][:].rearrange("p u n e -> p u (n e)").bitcast(F32).rearrange("p u (i r) -> p i u r", i=TT),
                     in_=bank[:],
@@ -209,7 +216,7 @@ def tile_coupledoscillatorrnntwosubsteps_d1p_kernel(
                 if q == "u":
                     lhsT, lhsT_scale, rhs, rhs_scale = vp[:, cols], scp[:, 1, cols], u_q[:, c, :], u_s[:, c, :]
                 else:
-                    lhsT, lhsT_scale = wp[:, q, cols], scp[4 * q : P, 0, cols]
+                    lhsT, lhsT_scale = wp[j // 4][:, q, 128 * (j % 4) : 128 * (j % 4) + 128], scp[4 * q : P, 0, cols]
                     rhs, rhs_scale = s_q[k, c][:, q, :], s_s[k, c][:, q, :]
                 nc.tensor.matmul_mx(
                     out=out, lhsT=lhsT.bitcast(FP8X4), lhsT_scale=lhsT_scale, rhs=rhs.bitcast(FP8X4), rhs_scale=rhs_scale,
@@ -249,8 +256,8 @@ def tile_coupledoscillatorrnntwosubsteps_d1p_kernel(
             for i in range(2):
                 m = mb[c, h, i] = psum.tile([P, 2, TC], F32, name="mb", bufs=4)
                 for e in range(2):
-                    nc.tensor.matmul(m[:, e, :], lhsT=eye75[:], rhs=raw[c, 2 + h][:, i, :, e], start=True, stop=False)
-                    nc.tensor.matmul(m[:, e, :], lhsT=eyem5[:], rhs=raw[c, h][:, i, :, e], start=False, stop=True)
+                    nc.tensor.matmul(m[:, e, :], lhsT=eye_z[:], rhs=raw[c, 2 + h][:, i, :, e], start=True, stop=False)
+                    nc.tensor.matmul(m[:, e, :], lhsT=eye_y[:], rhs=raw[c, h][:, i, :, e], start=False, stop=True)
 
         def state(c, h):
             z = z1[c, h] = sb("z1_%d%d" % (c, h), [P, 4, TC], F32)
@@ -260,18 +267,23 @@ def tile_coupledoscillatorrnntwosubsteps_d1p_kernel(
             for i in range(2):
                 pair = slice(2 * i, 2 * i + 2)
                 nc.vector.scalar_tensor_tensor(
-                    out=z[:, pair, :], in0=t1[c, h][:, pair, :], scalar=0.5, in1=mb[c, h, i][:], op0=ALU.mult, op1=ALU.add
+                    out=z[:, pair, :], in0=t1[c, h][:, pair, :], scalar=0.25, in1=mb[c, h, i][:], op0=ALU.mult, op1=ALU.add
                 )
-            for t in range(4):
-                nc.scalar.activation(out=zb[c, h][:, t, :], in_=z[:, t, :], func=ACT.Copy, scale=gf[:, 2 + h, t : t + 1])
             for i in range(2):
                 pair = slice(2 * i, 2 * i + 2)
-                nc.vector.scalar_tensor_tensor(
-                    out=y[:, pair, :], in0=z[:, pair, :], scalar=0.5,
-                    in1=raw[c, h][:, i].rearrange("p n e -> p e n"), op0=ALU.mult, op1=ALU.add,
+                nc.vector.tensor_tensor(
+                    out=y[:, pair, :], in0=z[:, pair, :], in1=raw[c, h][:, i].rearrange("p n e -> p e n"), op=ALU.add
                 )
+
+        def scale_z(c, h):
             for t in range(4):
-                nc.scalar.activation(out=yb[c, h][:, t, :], in_=y[:, t, :], func=ACT.Copy, scale=gf[:, h, t : t + 1])
+                nc.scalar.activation(
+                    out=zb[c, h][:, t, :], in_=z1[c, h][:, t, :], func=ACT.Copy, scale=gf[:, 2 + h, t : t + 1]
+                )
+
+        def scale_y(c, h):
+            for t in range(4):
+                nc.scalar.activation(out=yb[c, h][:, t, :], in_=y1[c, h][:, t, :], func=ACT.Copy, scale=gf[:, h, t : t + 1])
 
         def second_operand(c, h):
             sy = ring.tile([P, TC, 4], BF16, name="sy", align_bytes=64)
@@ -281,7 +293,14 @@ def tile_coupledoscillatorrnntwosubsteps_d1p_kernel(
             quantize(2, c, 2 + h, sz)
             quantize(2, c, h, sy)
 
-        y_half = sb("y_half", [P, 4, D], BF16)
+
+        def mean_velocity(c, h, pairs=(0, 1)):
+            for i in pairs:
+                pair = slice(2 * i, 2 * i + 2)
+                nc.vector.scalar_tensor_tensor(
+                    out=t2[c, h][:, pair, :], in0=t2[c, h][:, pair, :], scalar=0.5, in1=z1[c, h][:, pair, :],
+                    op0=ALU.mult, op1=ALU.add,
+                )
 
         def turn_y(n):
             c, h, i = units[n]
@@ -295,8 +314,7 @@ def tile_coupledoscillatorrnntwosubsteps_d1p_kernel(
             toks = slice(P * i, P * i + P)
             tz = turned_z[n] = psum.tile([P, 4, P], F32, name="tp", bufs=2)
             for t in range(4):
-                nc.tensor.matmul(tz[:, t, :], lhsT=z1[c, h][:, t, toks], rhs=ident[:], is_transpose=True, start=True, stop=False)
-                nc.tensor.matmul(tz[:, t, :], lhsT=t2[c, h][:, t, toks], rhs=ident[:], is_transpose=True, start=False, stop=True)
+                nc.tensor.transpose(tz[:, t, :], t2[c, h][:, t, toks], ident[:])
 
         z2 = {}
 
@@ -306,8 +324,9 @@ def tile_coupledoscillatorrnntwosubsteps_d1p_kernel(
             rows = slice(TC * c + P * i, TC * c + P * i + P)
             z2[n] = ring.tile([P, 512], F32, name="z2", bufs=4)
             nc.vector.scalar_tensor_tensor(
-                out=z2[n][:].rearrange("p (m t) -> p m t", t=4), in0=turned_z[n][:].rearrange("p t m -> p m t"), scalar=0.5,
-                in1=y_half[:, TT * c + i, cols].rearrange("p (m t) -> p m t", t=4), op0=ALU.mult, op1=ALU.subtract,
+                out=z2[n][:].rearrange("p (m t) -> p m t", t=4),
+                in0=y_nat[c, h][:, i, :].rearrange("p (m t) -> p m t", t=4), scalar=-0.5,
+                in1=turned_z[n][:].rearrange("p t m -> p m t"), op0=ALU.mult, op1=ALU.add,
             )
             nc.sync.dma_start(out=out_1[rows, cols], in_=z2[n][:])
 
@@ -326,52 +345,58 @@ def tile_coupledoscillatorrnntwosubsteps_d1p_kernel(
         turned_y = {}
         turned_z = {}
 
-        def half_y(i):
-            nc.vector.tensor_scalar(
-                out=y_half[:, i : i + 2, :], in0=y_nat[:, i : i + 2, :], scalar1=0.5, scalar2=None, op0=ALU.mult
-            )
-
         with tc.manual_schedule():
             transpose_in(0, (0, 1))
             cast_gain()
             gain_and_quantize(0, (0, 1))
+            transpose_in(0, (2, 3))
+            permute_scales(0, 0)
+            gain_and_quantize(0, (2, 3))
             widen_u(0)
             widen_u(1)
-            transpose_in(0, (2, 3))
-            half_y(0)
-            gain_and_quantize(0, (2, 3))
-            turn_u(0)
-            quantize_u(0)
             drift(0, 0)
+            turn_u(0)
+            drift(0, 1)
+            permute_w(0)
+            quantize_u(0)
+            permute_v(0)
+            permute_scales(1, 0)
+            cast_bias()
             widen_u(2)
             widen_u(3)
-            permute_w(0)
-            permute_scales(0)
-            permute_v(0)
-            cast_bias()
-            turn_u(1)
-            drift(0, 1)
             matmuls(1, 0, 0)
-            permute_w(1)
-            permute_scales(1)
+            permute_scales(0, 1)
+            permute_scales(1, 1)
             permute_v(1)
+            permute_w(1)
             transpose_in(1, (0, 1, 2, 3))
+            turn_u(1)
             state(0, 0)
-            matmuls(1, 0, 1)
+            scale_z(0, 0)
+            matmuls(1, 0, 1, pairs=(0,))
+            scale_y(0, 0)
+            matmuls(1, 0, 1, pairs=(1,))
             gain_and_quantize(1, (0, 1, 2, 3))
             quantize_u(1)
             second_operand(0, 0)
             matmuls(1, 1, 0)
             drift(1, 0)
             state(0, 1)
+            scale_z(0, 1)
+            scale_y(0, 1)
             matmuls(1, 1, 1)
             drift(1, 1)
             state(1, 0)
+            scale_z(1, 0)
+            scale_y(1, 0)
             second_operand(0, 1)
             matmuls(2, 0, 0, early=True)
             state(1, 1)
+            scale_z(1, 1)
+            scale_y(1, 1)
             second_operand(1, 0)
             matmuls(2, 0, 1)
+            mean_velocity(0, 0)
             for n in (0, 1):
                 turn_y(n)
                 turn_z(n)
@@ -380,18 +405,32 @@ def tile_coupledoscillatorrnntwosubsteps_d1p_kernel(
             finish_z(1)
             finish_y(0)
             finish_y(1)
+            mean_velocity(0, 1)
             matmuls(2, 1, 0, early=True)
-            half_y(2)
             for n in (2, 3):
                 turn_y(n)
                 turn_z(n)
             finish_z(2)
             finish_z(3)
+            mean_velocity(1, 0)
             finish_y(2)
             finish_y(3)
-            matmuls(2, 1, 1)
-            for n in range(4, 8):
+            matmuls(2, 1, 1, pairs=(0,))
+            for n in (4, 5):
                 turn_y(n)
                 turn_z(n)
-                finish_z(n)
-                finish_y(n)
+            matmuls(2, 1, 1, pairs=(1,))
+            finish_z(4)
+            finish_z(5)
+            mean_velocity(1, 1, pairs=(0,))
+            finish_y(4)
+            turn_y(6)
+            turn_y(7)
+            mean_velocity(1, 1, pairs=(1,))
+            finish_y(5)
+            turn_z(6)
+            finish_z(6)
+            turn_z(7)
+            finish_z(7)
+            finish_y(6)
+            finish_y(7)

@@ -232,7 +232,7 @@ def tile_coupledoscillatorrnntwosubsteps_d1p_kernel(
         yb = {}
         mb = {}
 
-        def matmuls(k, c, h, early=False, pairs=(0, 1)):
+        def matmuls(k, c, h, early=0, pairs=(0, 1)):
             if (k, c, h) in made:
                 t = made[k, c, h]
             elif k == 1:
@@ -242,12 +242,12 @@ def tile_coupledoscillatorrnntwosubsteps_d1p_kernel(
             made[k, c, h] = t
             banks = {i: psum.tile([P, 2, TC], F32, name="mx", bufs=2) for i in pairs}
             if early:
-                for i in range(2):
-                    mx_passes(banks[i][:, 0, :], 4 * h + 2 * i, k, c, ORDER[k][:3])
+                for i in pairs:
+                    mx_passes(banks[i][:, 0, :], 4 * h + 2 * i, k, c, ORDER[k][:early])
             for i in pairs:
                 bank = banks[i]
                 for e in range(2):
-                    mx_passes(bank[:, e, :], 4 * h + 2 * i + e, k, c, ORDER[k][3:] if early and e == 0 else ORDER[k])
+                    mx_passes(bank[:, e, :], 4 * h + 2 * i + e, k, c, ORDER[k][early:] if e == 0 else ORDER[k])
                 for e in range(2):
                     j = 4 * h + 2 * i + e
                     nc.scalar.activation(out=t[:, 2 * i + e, :], in_=bank[:, e, :], func=ACT.Tanh, bias=bf[:, j : j + 1])
@@ -350,7 +350,6 @@ def tile_coupledoscillatorrnntwosubsteps_d1p_kernel(
             cast_gain()
             gain_and_quantize(0, (0, 1))
             transpose_in(0, (2, 3))
-            permute_scales(0, 0)
             gain_and_quantize(0, (2, 3))
             widen_u(0)
             widen_u(1)
@@ -358,13 +357,14 @@ def tile_coupledoscillatorrnntwosubsteps_d1p_kernel(
             turn_u(0)
             drift(0, 1)
             permute_w(0)
+            permute_scales(0, 0)
             quantize_u(0)
             permute_v(0)
-            permute_scales(1, 0)
             cast_bias()
+            permute_scales(1, 0)
             widen_u(2)
             widen_u(3)
-            matmuls(1, 0, 0)
+            matmuls(1, 0, 0, early=4)
             permute_scales(0, 1)
             permute_scales(1, 1)
             permute_v(1)
@@ -390,7 +390,7 @@ def tile_coupledoscillatorrnntwosubsteps_d1p_kernel(
             scale_z(1, 0)
             scale_y(1, 0)
             second_operand(0, 1)
-            matmuls(2, 0, 0, early=True)
+            matmuls(2, 0, 0, early=3)
             state(1, 1)
             scale_z(1, 1)
             scale_y(1, 1)
@@ -406,7 +406,7 @@ def tile_coupledoscillatorrnntwosubsteps_d1p_kernel(
             finish_y(0)
             finish_y(1)
             mean_velocity(0, 1)
-            matmuls(2, 1, 0, early=True)
+            matmuls(2, 1, 0, early=3)
             for n in (2, 3):
                 turn_y(n)
                 turn_z(n)

from contextlib import ExitStack

import concourse.mybir as mybir
from concourse.masks import make_identity

N, D, E = 512, 1024, 512
D2 = 2 * D
FLOPS = 2 * N * D * (E + 2 * D2)

F32 = mybir.dt.float32
BF16 = mybir.dt.bfloat16
I32 = mybir.dt.int32
U8 = mybir.dt.uint8
FP8 = mybir.dt.float8_e4m3fn
FP8X4 = mybir.dt.float8_e4m3fn_x4
ALU = mybir.AluOpType
ACT = mybir.ActivationFunctionType

P = 128
TC = 256
CHUNKS = N // TC
TT = TC // P
ORDER = {1: (0, 1, 2, 3, "u"), 2: ("u", 0, 2, 1, 3)}


def tile_coupledoscillatorrnntwosubsteps_d1p_kernel(
    tc, y0, z0, u_bytes, u_scale, w_words, w_scales, v_words, v_scales, b, g, out_0, out_1
):
    nc = tc.nc
    with ExitStack() as ctx:
        keep = ctx.enter_context(tc.tile_pool(name="keep", bufs=1))
        ring = ctx.enter_context(tc.tile_pool(name="ring", bufs=2))
        psum = ctx.enter_context(tc.psum_pool(name="psum", bufs=1))

        def sb(name, shape, dtype):
            return keep.tile(shape, dtype, name=name, align_bytes=64)

        sc_raw = sb("sc_raw", [P, 2, D], U8)
        nc.vector.memset(sc_raw[:].rearrange("p x n -> p (x n)").bitcast(I32), 0)
        ident = sb("ident", [P, P], F32)
        make_identity(nc, ident[:])

        gb = sb("gb", [P, 4, 4], BF16)
        nc.scalar.dma_start(out=gb[:], in_=g.rearrange("(q p t) -> p q t", p=P, t=4))
        us = sb("us", [P, 4, 4], F32)
        nc.scalar.dma_start(out=us[:], in_=u_scale.rearrange("(i p) j -> p i j", p=P))
        bb = sb("bb", [P, 2, 4], BF16)

        w_raw = [sb("w_raw%d" % h, [P, 4, 512], I32) for h in range(2)]
        v_raw = sb("v_raw", [P, D], I32)
        w_view = w_words.rearrange("q p n t -> p q (n t)")
        v_view = v_words[0].rearrange("p n t -> p (n t)")
        y_view = y0.rearrange("(c i p) d -> p c i d", i=TT, p=P)
        z_view = z0.rearrange("(c i p) d -> p c i d", i=TT, p=P)
        y_nat = {(c, q): sb("y_nat%d%d" % (c, q), [P, TT, 512], BF16) for c in range(CHUNKS) for q in range(2)}
        z_nat = {(c, q): sb("z_nat%d%d" % (c, q), [P, TT, 512], BF16) for c in range(CHUNKS) for q in range(2)}

        def load_state(nat, view, c, q):
            nc.sync.dma_start(out=nat[c, q][:], in_=view[:, c, :, 512 * q : 512 * q + 512])
        u_raw = sb("u_raw", [P, 4, E], U8)

        def load_w(h, qs=slice(0, 4)):
            nc.sync.dma_start(
                out=w_raw[h][:, qs, :], in_=w_view[:, qs, 2048 * h : 2048 * h + 2048].bitcast(I32)
            )

        def load_w_scales(q):
            nc.sync.dma_start(
                out=sc_raw[32 * q : 32 * q + 16, 0, :].bitcast(I32), in_=w_scales[:, 4 * q : 4 * q + 4, :].bitcast(I32)
            )

        def load_v_scales(q):
            nc.sync.dma_start(
                out=sc_raw[32 * q : 32 * q + 4, 1, :].bitcast(I32), in_=v_scales[0, 4 * q : 4 * q + 4, :].bitcast(I32)
            )

        load_state(y_nat, y_view, 0, 0)
        load_state(y_nat, y_view, 0, 1)
        load_state(z_nat, z_view, 0, 0)
        load_state(z_nat, z_view, 0, 1)
        load_w_scales(0)
        load_w_scales(1)
        load_w_scales(2)
        load_w_scales(3)
        nc.sync.dma_start(out=u_raw[:], in_=u_bytes.rearrange("(i p) k -> p i k", p=P))
        load_w(0)
        load_v_scales(0)
        load_v_scales(1)
        load_v_scales(2)
        load_v_scales(3)
        nc.sync.dma_start(out=v_raw[:], in_=v_view.bitcast(I32))
        nc.sync.dma_start(out=bb[:], in_=b.rearrange("(q p t) -> p q t", p=P, t=4))
        load_w(1)
        load_state(y_nat, y_view, 1, 0)
        load_state(y_nat, y_view, 1, 1)
        load_state(z_nat, z_view, 1, 0)
        load_state(z_nat, z_view, 1, 1)

        eye_z = sb("eye_z", [P, P], BF16)
        nc.vector.tensor_scalar(out=eye_z[:], in0=ident[:], scalar1=0.375, scalar2=None, op0=ALU.mult)
        eye_y = sb("eye_y", [P, P], BF16)
        nc.vector.tensor_scalar(out=eye_y[:], in0=ident[:], scalar1=-0.25, scalar2=None, op0=ALU.mult)

        gf = sb("gf", [P, 4, 4], F32)
        bf = sb("bf", [P, 8], F32)

        def cast_gain():
            nc.vector.tensor_copy(out=gf[:, 0:2, :], in_=gb[:, 0:2, :])
            nc.vector.tensor_scalar(out=gf[:, 2:4, :], in0=gb[:, 2:4, :], scalar1=2.0, scalar2=None, op0=ALU.mult)

        def cast_bias():
            nc.vector.tensor_copy(out=bf[:], in_=bb[:].rearrange("p q t -> p (q t)"))

        def gain(q):
            return gb[:, q, :].rearrange("p (u e) -> p u e", e=2).unsqueeze(1).to_broadcast([P, TC, 2, 2])

        wp = [sb("wp%d" % h, [P, 4, 512], I32) for h in range(2)]
        vp = sb("vp", [P, D], I32)
        scp = sb("scp", [P, 2, D], U8)

        def permute_w(h, qs=slice(0, 4)):
            nc.vector.tensor_copy(
                out=wp[h][:, qs, :].rearrange("p q (t m) -> p q m t", t=4),
                in_=w_raw[h][:, qs, :].rearrange("p q (m t) -> p q m t", t=4),
            )

        def permute_scales(x, h):
            cols = slice(512 * h, 512 * h + 512)
            nc.vector.tensor_copy(
                out=scp[:, x, cols].rearrange("p (t m) -> p m t", t=4),
                in_=sc_raw[:, x, cols].rearrange("p (m t) -> p m t", t=4),
            )

        def permute_v(h):
            cols = slice(512 * h, 512 * h + 512)
            nc.vector.tensor_copy(
                out=vp[:, cols].rearrange("p (t m) -> p m t", t=4), in_=v_raw[:, cols].rearrange("p (m t) -> p m t", t=4)
            )

        u_wide = sb("u_wide", [P, 4, E], BF16)

        def widen_u(i):
            for j in range(4):
                nc.scalar.activation(
                    out=u_wide[:, i, 128 * j : 128 * j + 128],
                    in_=u_raw[:, i, 128 * j : 128 * j + 128].bitcast(FP8),
                    func=ACT.Copy,
                    scale=us[:, i, j : j + 1],
                )

        def words_transposed(nat):
            bank = psum.tile([P, TT, 2, P], F32, name="tp", bufs=2)
            for i in range(TT):
                words = nat[:, i, :].bitcast(F32)
                for e in range(2):
                    nc.tensor.transpose(bank[:, i, e, :], words[:, e::2], ident[:])
            return bank

        u_q = sb("u_q", [P, CHUNKS, TC], I32)
        u_s = sb("u_s", [P, CHUNKS, TC], U8)

        u_turned = {}

        def turn_u(c):
            ut = u_turned[c] = ring.tile([P, TC, 4], BF16, name="ut", align_bytes=64)
            bank = words_transposed(u_wide[:, TT * c : TT * c + TT, :])
            nc.scalar.copy(
                out=ut[:].rearrange("p (i r) t -> p i (r t)", i=TT).bitcast(F32).rearrange("p i (r e) -> p i r e", e=2),
                in_=bank[:].rearrange("p i e r -> p i r e"),
            )

        def quantize_u(c):
            nc.vector.quantize_mx(
                out=u_q[:, c, :].bitcast(FP8X4), scales=u_s[:, c, :], in_=u_turned[c][:].rearrange("p n t -> p (n t)")
            )

        raw = {}
        s_q = {}
        s_s = {}
        for k in (1, 2):
            for c in range(CHUNKS):
                s_q[k, c] = sb("sq%d%d" % (k, c), [P, 4, TC], I32)
                s_s[k, c] = sb("ss%d%d" % (k, c), [P, 4, TC], U8)

        def quantize(k, c, q, s):
            nc.vector.quantize_mx(
                out=s_q[k, c][:, q, :].bitcast(FP8X4), scales=s_s[k, c][:, q, :], in_=s[:].rearrange("p n t -> p (n t)")
            )

        def transpose_in(c, qs):
            for q in qs:
                nat = y_nat if q < 2 else z_nat
                raw[c, q] = sb("raw%d%d" % (c, q), [P, 2, TC, 2], BF16)
                bank = words_transposed(nat[c, q % 2])
                nc.scalar.copy(
                    out=raw[c, q][:].rearrange("p u n e -> p u (n e)").bitcast(F32).rearrange("p u (i r) -> p i u r", i=TT),
                    in_=bank[:],
                )

        def gain_and_quantize(c, qs):
            tiles = []
            for q in qs:
                s = ring.tile([P, TC, 4], BF16, name="s1", bufs=4, align_bytes=64)
                nc.vector.tensor_tensor(
                    out=s[:].rearrange("p n (u e) -> p n u e", e=2), in0=raw[c, q][:].rearrange("p u n e -> p n u e"),
                    in1=gain(q), op=ALU.mult,
                )
                tiles.append(s)
            for q, s in zip(qs, tiles):
                quantize(1, c, q, s)

        def mx_passes(out, j, k, c, passes):
            cols = slice(128 * j, 128 * j + 128)
            order = ORDER[k]
            for q in passes:
                if q == "u":
                    lhsT, lhsT_scale, rhs, rhs_scale = vp[:, cols], scp[:, 1, cols], u_q[:, c, :], u_s[:, c, :]
                else:
                    lhsT, lhsT_scale = wp[j // 4][:, q, 128 * (j % 4) : 128 * (j % 4) + 128], scp[4 * q : P, 0, cols]
                    rhs, rhs_scale = s_q[k, c][:, q, :], s_s[k, c][:, q, :]
                nc.tensor.matmul_mx(
                    out=out, lhsT=lhsT.bitcast(FP8X4), lhsT_scale=lhsT_scale, rhs=rhs.bitcast(FP8X4), rhs_scale=rhs_scale,
                    start=(q == order[0]), stop=(q == order[-1]),
                )

        made = {}
        t1 = {}
        z1 = {}
        y1 = {}
        t2 = {}
        zb = {}
        yb = {}
        mb = {}

        def matmuls(k, c, h, early=0, pairs=(0, 1)):
            if (k, c, h) in made:
                t = made[k, c, h]
            elif k == 1:
                t = t1[c, h] = ring.tile([P, 4, TC], F32, name="t1", bufs=4)
            else:
                t = t2[c, h] = sb("t2_%d%d" % (c, h), [P, 4, TC], F32)
            made[k, c, h] = t
            banks = {i: psum.tile([P, 2, TC], F32, name="mx", bufs=2) for i in pairs}
            if early:
                for i in pairs:
                    mx_passes(banks[i][:, 0, :], 4 * h + 2 * i, k, c, ORDER[k][:early])
            for i in pairs:
                bank = banks[i]
                for e in range(2):
                    mx_passes(bank[:, e, :], 4 * h + 2 * i + e, k, c, ORDER[k][early:] if e == 0 else ORDER[k])
                for e in range(2):
                    j = 4 * h + 2 * i + e
                    nc.scalar.activation(out=t[:, 2 * i + e, :], in_=bank[:, e, :], func=ACT.Tanh, bias=bf[:, j : j + 1])

        def drift(c, h):
            for i in range(2):
                m = mb[c, h, i] = psum.tile([P, 2, TC], F32, name="mb", bufs=4)
                for e in range(2):
                    nc.tensor.matmul(m[:, e, :], lhsT=eye_z[:], rhs=raw[c, 2 + h][:, i, :, e], start=True, stop=False)
                    nc.tensor.matmul(m[:, e, :], lhsT=eye_y[:], rhs=raw[c, h][:, i, :, e], start=False, stop=True)

        def state(c, h):
            z = z1[c, h] = sb("z1_%d%d" % (c, h), [P, 4, TC], F32)
            y = y1[c, h] = sb("y1_%d%d" % (c, h), [P, 4, TC], F32)
            zb[c, h] = ring.tile([P, 4, TC], BF16, name="zb")
            yb[c, h] = ring.tile([P, 4, TC], BF16, name="yb")
            for i in range(2):
                pair = slice(2 * i, 2 * i + 2)
                nc.vector.scalar_tensor_tensor(
                    out=z[:, pair, :], in0=t1[c, h][:, pair, :], scalar=0.25, in1=mb[c, h, i][:], op0=ALU.mult, op1=ALU.add
                )
            for i in range(2):
                pair = slice(2 * i, 2 * i + 2)
                nc.vector.tensor_tensor(
                    out=y[:, pair, :], in0=z[:, pair, :], in1=raw[c, h][:, i].rearrange("p n e -> p e n"), op=ALU.add
                )

        def scale_z(c, h):
            for t in range(4):
                nc.scalar.activation(
                    out=zb[c, h][:, t, :], in_=z1[c, h][:, t, :], func=ACT.Copy, scale=gf[:, 2 + h, t : t + 1]
                )

        def scale_y(c, h):
            for t in range(4):
                nc.scalar.activation(out=yb[c, h][:, t, :], in_=y1[c, h][:, t, :], func=ACT.Copy, scale=gf[:, h, t : t + 1])

        def second_operand(c, h):
            sy = ring.tile([P, TC, 4], BF16, name="sy", align_bytes=64)
            sz = ring.tile([P, TC, 4], BF16, name="sz", align_bytes=64)
            nc.vector.tensor_copy(out=sz[:], in_=zb[c, h][:].rearrange("p t n -> p n t"))
            nc.vector.tensor_copy(out=sy[:], in_=yb[c, h][:].rearrange("p t n -> p n t"))
            quantize(2, c, 2 + h, sz)
            quantize(2, c, h, sy)


        def mean_velocity(c, h, pairs=(0, 1)):
            for i in pairs:
                pair = slice(2 * i, 2 * i + 2)
                nc.vector.scalar_tensor_tensor(
                    out=t2[c, h][:, pair, :], in0=t2[c, h][:, pair, :], scalar=0.5, in1=z1[c, h][:, pair, :],
                    op0=ALU.mult, op1=ALU.add,
                )

        def turn_y(n):
            c, h, i = units[n]
            toks = slice(P * i, P * i + P)
            ty = turned_y[n] = psum.tile([P, 4, P], F32, name="mb", bufs=4)
            for t in range(4):
                nc.tensor.transpose(ty[:, t, :], y1[c, h][:, t, toks], ident[:])

        def turn_z(n):
            c, h, i = units[n]
            toks = slice(P * i, P * i + P)
            tz = turned_z[n] = psum.tile([P, 4, P], F32, name="tp", bufs=2)
            for t in range(4):
                nc.tensor.transpose(tz[:, t, :], t2[c, h][:, t, toks], ident[:])

        z2 = {}

        def finish_z(n):
            c, h, i = units[n]
            cols = slice(512 * h, 512 * h + 512)
            rows = slice(TC * c + P * i, TC * c + P * i + P)
            z2[n] = ring.tile([P, 512], F32, name="z2", bufs=4)
            nc.vector.scalar_tensor_tensor(
                out=z2[n][:].rearrange("p (m t) -> p m t", t=4),
                in0=y_nat[c, h][:, i, :].rearrange("p (m t) -> p m t", t=4), scalar=-0.5,
                in1=turned_z[n][:].rearrange("p t m -> p m t"), op0=ALU.mult, op1=ALU.add,
            )
            nc.sync.dma_start(out=out_1[rows, cols], in_=z2[n][:])

        def finish_y(n):
            c, h, i = units[n]
            cols = slice(512 * h, 512 * h + 512)
            rows = slice(TC * c + P * i, TC * c + P * i + P)
            y2 = ring.tile([P, 512], F32, name="y2", bufs=4)
            nc.vector.scalar_tensor_tensor(
                out=y2[:].rearrange("p (m t) -> p m t", t=4), in0=z2[n][:].rearrange("p (m t) -> p m t", t=4), scalar=0.5,
                in1=turned_y[n][:].rearrange("p t m -> p m t"), op0=ALU.mult, op1=ALU.add,
            )
            nc.sync.dma_start(out=out_0[rows, cols], in_=y2[:])

        units = [(c, h, i) for c in range(CHUNKS) for h in range(2) for i in range(TT)]
        turned_y = {}
        turned_z = {}

        with tc.manual_schedule():
            transpose_in(0, (0, 1))
            cast_gain()
            gain_and_quantize(0, (0, 1))
            transpose_in(0, (2, 3))
            gain_and_quantize(0, (2, 3))
            widen_u(0)
            widen_u(1)
            drift(0, 0)
            turn_u(0)
            drift(0, 1)
            permute_w(0)
            permute_scales(0, 0)
            quantize_u(0)
            permute_v(0)
            cast_bias()
            permute_scales(1, 0)
            widen_u(2)
            widen_u(3)
            matmuls(1, 0, 0, early=4)
            permute_scales(0, 1)
            permute_scales(1, 1)
            permute_v(1)
            permute_w(1)
            transpose_in(1, (0, 1, 2, 3))
            turn_u(1)
            state(0, 0)
            scale_z(0, 0)
            matmuls(1, 0, 1, pairs=(0,))
            scale_y(0, 0)
            matmuls(1, 0, 1, pairs=(1,))
            gain_and_quantize(1, (0, 1, 2, 3))
            quantize_u(1)
            second_operand(0, 0)
            matmuls(1, 1, 0)
            drift(1, 0)
            state(0, 1)
            scale_z(0, 1)
            scale_y(0, 1)
            matmuls(1, 1, 1)
            drift(1, 1)
            state(1, 0)
            scale_z(1, 0)
            scale_y(1, 0)
            second_operand(0, 1)
            matmuls(2, 0, 0, early=3)
            state(1, 1)
            scale_z(1, 1)
            scale_y(1, 1)
            second_operand(1, 0)
            matmuls(2, 0, 1)
            mean_velocity(0, 0)
            for n in (0, 1):
                turn_y(n)
                turn_z(n)
            second_operand(1, 1)
            finish_z(0)
            finish_z(1)
            finish_y(0)
            finish_y(1)
            mean_velocity(0, 1)
            matmuls(2, 1, 0, early=3)
            for n in (2, 3):
                turn_y(n)
                turn_z(n)
            finish_z(2)
            finish_z(3)
            mean_velocity(1, 0)
            finish_y(2)
            finish_y(3)
            matmuls(2, 1, 1, pairs=(0,))
            for n in (4, 5):
                turn_y(n)
                turn_z(n)
            matmuls(2, 1, 1, pairs=(1,))
            finish_z(4)
            finish_z(5)
            mean_velocity(1, 1, pairs=(0,))
            finish_y(4)
            turn_y(6)
            turn_y(7)
            mean_velocity(1, 1, pairs=(1,))
            finish_y(5)
            turn_z(6)
            finish_z(6)
            turn_z(7)
            finish_z(7)
            finish_y(6)
            finish_y(7)
